import numpy as np
import ml_dtypes


def mxq(x, axis, fmt="e4m3"):
    dtype, down = {"e4m3": (ml_dtypes.float8_e4m3fn, 7), "e5m2": (ml_dtypes.float8_e5m2, 14)}[fmt]
    v = np.moveaxis(np.asarray(x, np.float32).astype(ml_dtypes.bfloat16).astype(np.float64), axis, -1)
    blocks = v.reshape(v.shape[:-1] + (-1, 32))
    amax = np.abs(blocks).max(-1, keepdims=True)
    byte = np.maximum(np.where(amax > 0, np.frexp(amax)[1] - 1 + 127, 0) - down, 1)
    scale = np.exp2(byte - 127.0)
    codes = (blocks / scale).astype(np.float32).astype(dtype).astype(np.float64)
    return np.moveaxis((codes * scale).reshape(v.shape), -1, axis)


WIDE = False


def mx_kscale(k):
    if not WIDE:
        return np.ones(k)
    levels = np.array([10, -10, 5, -5, 0])
    if k % 512:
        return np.exp2(np.random.permutation(np.resize(levels, k // 32))).repeat(32)
    a = np.empty((k // 512, 16))
    for p in range(k // 512):
        a[p, :8] = np.random.permutation(np.resize(levels, 8))
        for g in range(8):
            far = levels[np.abs(levels - a[p, g]) >= 10]
            a[p, g + 8] = far[np.random.randint(len(far))]
    return np.exp2(a.ravel()).repeat(32)


def f64(x):
    return np.asarray(x).astype(np.float64)


def striped(idx):
    return np.tile(idx.reshape(-1, 16).T, (8, 1)).astype(np.uint16)


def unstriped(offs):
    return offs[:16].T.reshape(-1).astype(np.int64)


def striped8(idx):
    return np.concatenate([x.reshape(-1, 16).T for x in idx]).astype(np.uint16)


def runs(offs, k):
    lists = np.stack([offs[16 * r : 16 * r + 16].T.reshape(-1) for r in range(8)]).astype(np.int64)
    return lists[np.arange(k) % 512 // 64]


def pack_weight(w):
    k, n = w.shape
    w = f64(np.asarray(w, np.float32).astype(ml_dtypes.bfloat16)).reshape(k // 32, 32, n)
    amax = np.abs(w).max(1)
    byte = np.clip(np.where(amax > 0, np.frexp(amax)[1] - 1 + 127 - 7, 1), 1, 254)
    scaled = (w * np.exp2(127.0 - byte)[:, None, :]).reshape(k, n).astype(np.float32)
    words = np.ascontiguousarray(scaled.reshape(k // 512, 128, 4, n).transpose(0, 1, 3, 2)).astype(ml_dtypes.float8_e4m3fn).view(np.uint8)
    return words, np.ascontiguousarray(byte.astype(np.uint8).reshape(k // 512, 16, n))


def unpack_weight(words, scales):
    g, p, n, _ = words.shape
    vals = np.ascontiguousarray(words).view(ml_dtypes.float8_e4m3fn).astype(np.float64) * np.repeat(np.exp2(scales.astype(np.float64) - 127.0), 8, axis=1)[..., None]
    return vals.transpose(0, 1, 3, 2).reshape(g * 512, n)


E2M1 = np.array([0.0, 0.5, 1.0, 1.5, 2.0, 3.0, 4.0, 6.0, -0.0, -0.5, -1.0, -1.5, -2.0, -3.0, -4.0, -6.0])


def pack_fp4(w):
    k, n = w.shape
    w = f64(np.asarray(w, np.float32).astype(ml_dtypes.bfloat16)).reshape(k // 32, 32, n)
    amax = np.abs(w).max(1)
    mant, ex = np.frexp(amax / 6.0)
    byte = np.clip(np.where(amax > 0, np.where(mant > 0.5, ex, ex - 1) + 127, 1), 1, 254)
    scaled = (w * np.exp2(127.0 - byte)[:, None, :]).reshape(k, n).astype(np.float32)
    c = np.ascontiguousarray(scaled.reshape(k // 512, 128, 4, n).transpose(0, 1, 3, 2)).astype(ml_dtypes.float4_e2m1fn).view(np.uint8) & 0xF
    words = (c[..., 0::2] | (c[..., 1::2] << 4)).reshape(k // 512, 128, 2 * n)
    return np.ascontiguousarray(words), np.ascontiguousarray(byte.astype(np.uint8).reshape(k // 512, 16, n))


def unpack_fp4(words, scales):
    g, _, n = scales.shape
    words = np.ascontiguousarray(words).reshape(g, 128, n, 2)
    nib = np.empty((g, 128, n, 4), np.uint8)
    nib[..., 0::2] = words & 0xF
    nib[..., 1::2] = words >> 4
    vals = E2M1[nib] * np.repeat(np.exp2(scales.astype(np.float64) - 127.0), 8, axis=1)[..., None]
    return vals.transpose(0, 1, 3, 2).reshape(g * 512, n)


def sigmoid(v):
    return 1.0 / (1.0 + np.exp(-np.maximum(v, -700.0)))


K, T, S, N, G, H, W = 512, 1024, 512, 512, 2048, 512, 256


def setup_inputs():
    n = np.random.standard_normal
    s = mx_kscale(K)[:, None]
    u = mx_kscale(S)
    packed_xT = pack_weight(n((K, T)) * s)
    packed_dT = pack_weight(n((K, G)) / s)
    packed_w1 = pack_fp4(n((H, N)) / np.sqrt(2 * H) / u[:, None])
    packed_w2 = pack_fp4(n((K, N)) / np.sqrt(2 * K) / s)
    perm = np.random.permutation(S)
    return {
        "x_words": packed_xT[0],
        "x_scales": packed_xT[1],
        "d_words": packed_dT[0],
        "d_scales": packed_dT[1],
        "sl": np.random.uniform(1.0, 2.0, (H, 1)).astype(np.float32),
        "th": (0.5 * n((H, 1))).astype(np.float32),
        "gn": (np.random.uniform(0.5, 1.5, (H, 1)) * u[:, None]).astype(np.float32),
        "w1_words": packed_w1[0],
        "w1_scales": packed_w1[1],
        "w2_words": packed_w2[0],
        "w2_scales": packed_w2[1],
        "offs": striped(np.random.permutation(T)[:S]),
        "ci": striped(np.random.permutation(G)[:H]),
        "n1": striped8(np.stack([np.random.permutation(S) for _ in range(8)])),
        "n2": striped8(np.stack([np.random.permutation(S) for _ in range(8)])),
        "two": striped(np.random.permutation(T)[:S]),
        "n3": striped(perm[:W]),
        "n4": striped(perm[W:]),
        "n5": striped(np.random.permutation(S)),
    }


def reference(x_words, x_scales, d_words, d_scales, sl, th, gn, w1_words, w1_scales, w2_words, w2_scales, offs, ci, n1, n2, two, n3, n4, n5):
    d_ci = unpack_weight(d_words, d_scales)[:, unstriped(ci)]
    xq = unpack_weight(x_words, x_scales)[:, unstriped(offs)]
    s = 0.0625 * (d_ci.T @ xq)
    sg = sigmoid(f64(sl) * (s[np.arange(H)[:, None], runs(n1, H)] - f64(th)))
    z = f64(gn) * ((s[np.arange(H)[:, None], runs(n2, H)]) * sg)
    x_two = unpack_weight(x_words, x_scales)[:, unstriped(two)]
    h = unpack_fp4(w1_words, w1_scales).T @ mxq(z, 0, "e4m3") + unpack_fp4(w2_words, w2_scales).T @ x_two
    pa = h[:, unstriped(n3)]
    pb = h[:, unstriped(n4)]
    ra = np.maximum(pa, pb)
    ds = h.copy()
    ds[:, unstriped(n3)] = ra
    return ds - ds[:, unstriped(n5)]

@@ -1,0 +1,219 @@
+from contextlib import ExitStack
+
+import concourse.mybir as mybir
+
+K, T, S, N, G, H, W = 512, 1024, 512, 512, 2048, 512, 256
+FLOPS = 3 * 2 * 512 * 512 * 512
+
+F32 = mybir.dt.float32
+BF16 = mybir.dt.bfloat16
+I32 = mybir.dt.int32
+U32 = mybir.dt.uint32
+U16 = mybir.dt.uint16
+U8 = mybir.dt.uint8
+FP8X4 = mybir.dt.float8_e4m3fn_x4
+FP4X4 = mybir.dt.float4_e2m1fn_x4
+ALU = mybir.AluOpType
+ACT = mybir.ActivationFunctionType
+
+P = 128
+PACK = 4
+HALF = S // 2
+
+
+def tile_picked_dwmemgfillm_none_p_kernel(
+    tc, x_words, x_scales, d_words, d_scales, sl, th, gn, w1_words, w1_scales, w2_words, w2_scales,
+    offs, ci, n1, n2, two, n3, n4, n5, out,
+):
+    nc = tc.nc
+    with ExitStack() as ctx:
+        keep = ctx.enter_context(tc.tile_pool(name="keep", bufs=1))
+        psum = ctx.enter_context(tc.psum_pool(name="psum", bufs=1))
+
+        def load_list(src, name):
+            lst = keep.tile(list(src.shape), U16, name=name)
+            nc.sync.dma_start(lst[:], src)
+            return lst
+
+        def scale_tile(src, name):
+            plane = keep.tile([P, src.shape[2]], U8, name=name, align_bytes=64)
+            nc.vector.memset(plane[:].bitcast(I32), 0)
+            return plane
+
+        def load_scales(queue, plane, src):
+            for q in range(4):
+                queue.dma_start(plane[32 * q : 32 * q + 4, :].bitcast(I32), src[0, 4 * q : 4 * q + 4, :].bitcast(I32))
+
+        def load_fp8_words(src, name):
+            words = keep.tile([P, src.shape[2]], U32, name=name, align_bytes=64)
+            nc.sync.dma_start(words[:].bitcast(I32), src[0].rearrange("p n t -> p (n t)").bitcast(I32))
+            return words
+
+        def load_fp4_words(src, name):
+            words = keep.tile([P, src.shape[2]], U8, name=name, align_bytes=64)
+            nc.sync.dma_start(words[:].bitcast(I32), src[0].bitcast(I32))
+            return words
+
+        def load_rows(src, name):
+            col = keep.tile([P, PACK], F32, name=name)
+            nc.gpsimd.dma_start(col[:], src.rearrange("(p t) o -> p (t o)", t=PACK))
+            return col
+
+        x_sc = scale_tile(x_scales, "x_sc")
+        d_sc = scale_tile(d_scales, "d_sc")
+        w2_sc = scale_tile(w2_scales, "w2_sc")
+        w1_sc = scale_tile(w1_scales, "w1_sc")
+
+        offs_l = load_list(offs, "offs_l")
+        ci_l = load_list(ci, "ci_l")
+        n1_l = load_list(n1, "n1_l")
+        load_scales(nc.sync, x_sc, x_scales)
+        x_w = load_fp8_words(x_words, "x_w")
+        load_scales(nc.sync, d_sc, d_scales)
+        d_w = load_fp8_words(d_words, "d_w")
+        two_l = load_list(two, "two_l")
+        n2_l = load_list(n2, "n2_l")
+        load_scales(nc.sync, w2_sc, w2_scales)
+        w2_w = load_fp4_words(w2_words, "w2_w")
+        load_scales(nc.sync, w1_sc, w1_scales)
+        w1_w = load_fp4_words(w1_words, "w1_w")
+        n3_l = load_list(n3, "n3_l")
+        n4_l = load_list(n4, "n4_l")
+        n5_l = load_list(n5, "n5_l")
+        sl_t = load_rows(sl, "sl_t")
+        th_t = load_rows(th, "th_t")
+        gn_t = load_rows(gn, "gn_t")
+        sl_th = keep.tile([P, PACK], F32)
+        bias = keep.tile([P, PACK], F32)
+        nc.gpsimd.tensor_tensor(sl_th[:], sl_t[:], th_t[:], ALU.mult)
+        nc.gpsimd.tensor_scalar(out=bias[:], in0=sl_th[:], scalar1=-1.0, scalar2=0.0, op0=ALU.mult, op1=ALU.add)
+
+        xq_s = keep.tile([P, S], U8, align_bytes=64)
+        xq_w = keep.tile([P, S], U32, align_bytes=64)
+        dq_s = keep.tile([P, H], U8, align_bytes=64)
+        dq_w = keep.tile([P, H], U32, align_bytes=64)
+        x2_s = keep.tile([P, S], U8, align_bytes=64)
+        x2_w = keep.tile([P, S], U32, align_bytes=64)
+        nc.vector.tensor_copy(xq_s[:], x_sc[:].indirect(offs_l[:]))
+        nc.vector.tensor_copy(xq_w[:], x_w[:].indirect(offs_l[:]))
+        nc.vector.tensor_copy(dq_s[:].rearrange("p (t m) -> p m t", t=PACK), d_sc[:].indirect(ci_l[:]))
+        nc.vector.tensor_copy(dq_w[:].rearrange("p (t m) -> p m t", t=PACK), d_w[:].indirect(ci_l[:]))
+        nc.vector.tensor_copy(x2_s[:], x_sc[:].indirect(two_l[:]))
+        nc.vector.tensor_copy(x2_w[:], x_w[:].indirect(two_l[:]))
+
+        s_bank = [psum.tile([P, S], F32, name=f"s_bank{t}") for t in range(PACK)]
+        h_bank = [psum.tile([P, S], F32, name=f"h_bank{b}") for b in range(N // P)]
+        for t in range(PACK):
+            cols = slice(P * t, P * (t + 1))
+            nc.tensor.matmul_mx(
+                out=s_bank[t][:], lhsT=dq_w[:, cols].bitcast(FP8X4), lhsT_scale=dq_s[:, cols],
+                rhs=xq_w[:].bitcast(FP8X4), rhs_scale=xq_s[:], start=True, stop=True,
+            )
+        for b in range(N // P):
+            nc.tensor.matmul_mx(
+                out=h_bank[b][:], lhsT=w2_w[:, 2 * P * b : 2 * P * (b + 1)].bitcast(FP4X4), lhsT_scale=w2_sc[:, P * b : P * (b + 1)],
+                rhs=x2_w[:].bitcast(FP8X4), rhs_scale=x2_s[:], start=True, stop=False,
+            )
+
+        s = [keep.tile([P, S], F32, name=f"s{t}") for t in range(PACK)]
+        gs = [keep.tile([P, S], F32, name=f"gs{t}") for t in range(PACK)]
+        sg = [[keep.tile([P, HALF], F32, name=f"sg{a}_{t}") for t in range(PACK)] for a in range(2)]
+        z = [keep.tile([P, PACK, HALF], F32, name=f"z{a}") for a in range(2)]
+        zb = [keep.tile([P, HALF, PACK], BF16, name=f"zb{a}", align_bytes=64) for a in range(2)]
+        zq_w = keep.tile([P, S], U32, align_bytes=64)
+        zq_s = keep.tile([P, S], U8, align_bytes=64)
+
+        def half_list(lst, a):
+            return lst[:, a * HALF // 16 : (a + 1) * HALF // 16]
+
+        def gate(a, t):
+            nc.scalar.activation(out=sg[a][t][:], in_=s[t][:].indirect(half_list(n1_l, a)), func=ACT.Sigmoid,
+                                 scale=sl_t[:, t : t + 1], bias=bias[:, t : t + 1])
+
+        def product(a, t):
+            nc.vector.tensor_tensor(z[a][:, t, :], gs[t][:].indirect(half_list(n2_l, a)), sg[a][t][:], ALU.mult)
+
+        def weave(copy, a):
+            copy(zb[a][:].rearrange("p (c i) t -> p c t i", i=4), z[a][:].rearrange("p t (c i) -> p c t i", i=4))
+
+        def quantise(a):
+            cols = slice(a * HALF, (a + 1) * HALF)
+            nc.vector.quantize_mx(out=zq_w[:, cols].bitcast(FP8X4), scales=zq_s[:, cols], in_=zb[a][:].rearrange("p c t -> p (c t)"))
+
+        for t in range(PACK):
+            nc.scalar.activation(out=s[t][:], in_=s_bank[t][:], func=ACT.Copy, scale=0.0625)
+            gate(0, t)
+            nc.vector.tensor_scalar(out=gs[t][:], in0=s[t][:], scalar1=gn_t[:, t : t + 1], scalar2=None, op0=ALU.mult)
+            product(0, t)
+        for t in range(PACK):
+            gate(1, t)
+            product(1, t)
+        weave(nc.scalar.copy, 0)
+        weave(nc.vector.tensor_copy, 1)
+        quantise(0)
+        quantise(1)
+
+        for a in range(2):
+            cols = slice(a * HALF, (a + 1) * HALF)
+            for b in range(N // P):
+                nc.tensor.matmul_mx(
+                    out=h_bank[b][:, cols], lhsT=w1_w[:, 2 * P * b : 2 * P * (b + 1)].bitcast(FP4X4), lhsT_scale=w1_sc[:, P * b : P * (b + 1)],
+                    rhs=zq_w[:, cols].bitcast(FP8X4), rhs_scale=zq_s[:, cols], start=False, stop=(a == 1),
+                )
+
+        ds = [keep.tile([P, S], F32, name=f"ds{b}") for b in range(4)]
+        pa = [keep.tile([P, W], F32, name=f"pa{b}") for b in range(4)]
+        pb = [keep.tile([P, W], F32, name=f"pb{b}") for b in range(4)]
+        ra = [keep.tile([P, W], F32, name=f"ra{b}") for b in range(4)]
+        aux = [keep.tile([P, S], F32, name=f"aux{b}") for b in range(4)]
+        res = [[keep.tile([P, HALF], F32, name=f"res{b}_{a}") for a in range(2)] for b in range(4)]
+
+        def v_gather(o, win):
+            nc.vector.tensor_copy(o, win)
+
+        def s_gather(o, win):
+            nc.scalar.activation(out=o, in_=win, func=ACT.Copy)
+
+        def larger(b):
+            nc.vector.tensor_tensor(ra[b][:], pa[b][:], pb[b][:], ALU.max)
+
+        def put(b):
+            nc.scalar.activation(out=ds[b][:].indirect(n3_l[:]), in_=ra[b][:], func=ACT.Copy)
+
+        def store(b, a):
+            nc.sync.dma_start(out[P * b : P * (b + 1), a * HALF : (a + 1) * HALF], res[b][a][:])
+
+        def finish_fused(b):
+            nc.vector.tensor_scalar(out=aux[b][:], in0=ds[b][:], scalar1=-1.0, scalar2=None, op0=ALU.mult)
+            for a in range(2):
+                nc.vector.tensor_tensor(res[b][a][:], aux[b][:].indirect(half_list(n5_l, a)), ds[b][:, a * HALF : (a + 1) * HALF], ALU.add)
+                store(b, a)
+
+        def finish_split(b):
+            for a in range(2):
+                cols = slice(a * HALF, (a + 1) * HALF)
+                s_gather(aux[b][:, cols], ds[b][:].indirect(half_list(n5_l, a)))
+                nc.vector.tensor_tensor(res[b][a][:], ds[b][:, cols], aux[b][:, cols], ALU.subtract)
+                store(b, a)
+
+        nc.scalar.copy(ds[0][:], h_bank[0][:])
+        nc.vector.tensor_copy(ds[1][:], h_bank[1][:])
+        s_gather(pa[0][:], ds[0][:].indirect(n3_l[:]))
+        v_gather(pb[0][:], ds[0][:].indirect(n4_l[:]))
+        larger(0)
+        nc.scalar.copy(ds[2][:], h_bank[2][:])
+        put(0)
+        v_gather(pa[1][:], ds[1][:].indirect(n3_l[:]))
+        v_gather(pb[1][:], ds[1][:].indirect(n4_l[:]))
+        larger(1)
+        put(1)
+        nc.vector.tensor_copy(ds[3][:], h_bank[3][:])
+        for b in (2, 3):
+            v_gather(pa[b][:], ds[b][:].indirect(n3_l[:]))
+            v_gather(pb[b][:], ds[b][:].indirect(n4_l[:]))
+            larger(b)
+            put(b)
+        finish_fused(0)
+        finish_fused(1)
+        finish_fused(2)
+        finish_split(3)

@@ -35,9 +35,9 @@ def tile_picked_dwmemgfillm_none_p_kernel(
             nc.sync.dma_start(lst[:], src)
             return lst
 
-        def scale_tile(src, name):
+        def scale_tile(engine, src, name):
             plane = keep.tile([P, src.shape[2]], U8, name=name, align_bytes=64)
-            nc.vector.memset(plane[:].bitcast(I32), 0)
+            engine.memset(plane[:].bitcast(I32), 0)
             return plane
 
         def load_scales(queue, plane, src):
@@ -59,10 +59,10 @@ def tile_picked_dwmemgfillm_none_p_kernel(
             nc.gpsimd.dma_start(col[:], src.rearrange("(p t) o -> p (t o)", t=PACK))
             return col
 
-        x_sc = scale_tile(x_scales, "x_sc")
-        d_sc = scale_tile(d_scales, "d_sc")
-        w2_sc = scale_tile(w2_scales, "w2_sc")
-        w1_sc = scale_tile(w1_scales, "w1_sc")
+        x_sc = scale_tile(nc.vector, x_scales, "x_sc")
+        d_sc = scale_tile(nc.vector, d_scales, "d_sc")
+        w2_sc = scale_tile(nc.vector, w2_scales, "w2_sc")
+        w1_sc = scale_tile(nc.vector, w1_scales, "w1_sc")
 
         offs_l = load_list(offs, "offs_l")
         ci_l = load_list(ci, "ci_l")
@@ -86,7 +86,7 @@ def tile_picked_dwmemgfillm_none_p_kernel(
         sl_th = keep.tile([P, PACK], F32)
         bias = keep.tile([P, PACK], F32)
         nc.gpsimd.tensor_tensor(sl_th[:], sl_t[:], th_t[:], ALU.mult)
-        nc.gpsimd.tensor_scalar(out=bias[:], in0=sl_th[:], scalar1=-1.0, scalar2=0.0, op0=ALU.mult, op1=ALU.add)
+        nc.scalar.activation(out=bias[:], in_=sl_th[:], func=ACT.Copy, scale=-1.0)
 
         xq_s = keep.tile([P, S], U8, align_bytes=64)
         xq_w = keep.tile([P, S], U32, align_bytes=64)
@@ -99,7 +99,6 @@ def tile_picked_dwmemgfillm_none_p_kernel(
         nc.vector.tensor_copy(dq_s[:].rearrange("p (t m) -> p m t", t=PACK), d_sc[:].indirect(ci_l[:]))
         nc.vector.tensor_copy(dq_w[:].rearrange("p (t m) -> p m t", t=PACK), d_w[:].indirect(ci_l[:]))
         nc.vector.tensor_copy(x2_s[:], x_sc[:].indirect(two_l[:]))
-        nc.vector.tensor_copy(x2_w[:], x_w[:].indirect(two_l[:]))
 
         s_bank = [psum.tile([P, S], F32, name=f"s_bank{t}") for t in range(PACK)]
         h_bank = [psum.tile([P, S], F32, name=f"h_bank{b}") for b in range(N // P)]
@@ -108,11 +107,6 @@ def tile_picked_dwmemgfillm_none_p_kernel(
             nc.tensor.matmul_mx(
                 out=s_bank[t][:], lhsT=dq_w[:, cols].bitcast(FP8X4), lhsT_scale=dq_s[:, cols],
                 rhs=xq_w[:].bitcast(FP8X4), rhs_scale=xq_s[:], start=True, stop=True,
-            )
-        for b in range(N // P):
-            nc.tensor.matmul_mx(
-                out=h_bank[b][:], lhsT=w2_w[:, 2 * P * b : 2 * P * (b + 1)].bitcast(FP4X4), lhsT_scale=w2_sc[:, P * b : P * (b + 1)],
-                rhs=x2_w[:].bitcast(FP8X4), rhs_scale=x2_s[:], start=True, stop=False,
             )
 
         s = [keep.tile([P, S], F32, name=f"s{t}") for t in range(PACK)]
@@ -140,32 +134,42 @@ def tile_picked_dwmemgfillm_none_p_kernel(
             cols = slice(a * HALF, (a + 1) * HALF)
             nc.vector.quantize_mx(out=zq_w[:, cols].bitcast(FP8X4), scales=zq_s[:, cols], in_=zb[a][:].rearrange("p c t -> p (c t)"))
 
+        nc.vector.tensor_copy(x2_w[:], x_w[:].indirect(two_l[:]))
+        for b in range(N // P):
+            nc.tensor.matmul_mx(
+                out=h_bank[b][:], lhsT=w2_w[:, 2 * P * b : 2 * P * (b + 1)].bitcast(FP4X4), lhsT_scale=w2_sc[:, P * b : P * (b + 1)],
+                rhs=x2_w[:].bitcast(FP8X4), rhs_scale=x2_s[:], start=True, stop=False,
+            )
+        def s_leaves_psum(t):
+            if t < 2:
+                nc.scalar.activation(out=s[t][:], in_=s_bank[t][:], func=ACT.Copy, scale=0.0625)
+            else:
+                nc.vector.tensor_scalar(out=s[t][:], in0=s_bank[t][:], scalar1=0.0625, scalar2=None, op0=ALU.mult)
+            nc.gpsimd.tensor_scalar(out=gs[t][:], in0=s[t][:], scalar1=gn_t[:, t : t + 1], scalar2=0.0, op0=ALU.mult, op1=ALU.add)
+
         for t in range(PACK):
-            nc.scalar.activation(out=s[t][:], in_=s_bank[t][:], func=ACT.Copy, scale=0.0625)
-            gate(0, t)
-            nc.vector.tensor_scalar(out=gs[t][:], in0=s[t][:], scalar1=gn_t[:, t : t + 1], scalar2=None, op0=ALU.mult)
-            product(0, t)
-        for t in range(PACK):
-            gate(1, t)
-            product(1, t)
+            s_leaves_psum(t)
+        for a, t in ((0, 0), (1, 0), (0, 1), (1, 1), (0, 2), (0, 3), (1, 2), (1, 3)):
+            gate(a, t)
+            product(a, t)
         weave(nc.scalar.copy, 0)
         weave(nc.vector.tensor_copy, 1)
         quantise(0)
         quantise(1)
 
-        for a in range(2):
-            cols = slice(a * HALF, (a + 1) * HALF)
-            for b in range(N // P):
+        for b in range(N // P):
+            for a in range(2):
+                cols = slice(a * HALF, (a + 1) * HALF)
                 nc.tensor.matmul_mx(
                     out=h_bank[b][:, cols], lhsT=w1_w[:, 2 * P * b : 2 * P * (b + 1)].bitcast(FP4X4), lhsT_scale=w1_sc[:, P * b : P * (b + 1)],
                     rhs=zq_w[:, cols].bitcast(FP8X4), rhs_scale=zq_s[:, cols], start=False, stop=(a == 1),
                 )
 
         ds = [keep.tile([P, S], F32, name=f"ds{b}") for b in range(4)]
+        ra = [keep.tile([P, W], F32, name=f"ra{b}") for b in range(4)]
         pa = [keep.tile([P, W], F32, name=f"pa{b}") for b in range(4)]
         pb = [keep.tile([P, W], F32, name=f"pb{b}") for b in range(4)]
-        ra = [keep.tile([P, W], F32, name=f"ra{b}") for b in range(4)]
-        aux = [keep.tile([P, S], F32, name=f"aux{b}") for b in range(4)]
+        far = [[keep.tile([P, HALF], F32, name=f"far{b}_{a}") for a in range(2)] for b in range(4)]
         res = [[keep.tile([P, HALF], F32, name=f"res{b}_{a}") for a in range(2)] for b in range(4)]
 
         def v_gather(o, win):
@@ -174,46 +178,53 @@ def tile_picked_dwmemgfillm_none_p_kernel(
         def s_gather(o, win):
             nc.scalar.activation(out=o, in_=win, func=ACT.Copy)
 
+        def fetch_a(b):
+            v_gather(pa[b][:], ds[b][:].indirect(n3_l[:]))
+
+        def fetch_b(b):
+            v_gather(pb[b][:], ds[b][:].indirect(n4_l[:]))
+
         def larger(b):
             nc.vector.tensor_tensor(ra[b][:], pa[b][:], pb[b][:], ALU.max)
 
         def put(b):
             nc.scalar.activation(out=ds[b][:].indirect(n3_l[:]), in_=ra[b][:], func=ACT.Copy)
 
-        def store(b, a):
-            nc.sync.dma_start(out[P * b : P * (b + 1), a * HALF : (a + 1) * HALF], res[b][a][:])
+        def fetch(gather, b, a):
+            gather(far[b][a][:], ds[b][:].indirect(half_list(n5_l, a)))
 
-        def finish_fused(b):
-            nc.vector.tensor_scalar(out=aux[b][:], in0=ds[b][:], scalar1=-1.0, scalar2=None, op0=ALU.mult)
-            for a in range(2):
-                nc.vector.tensor_tensor(res[b][a][:], aux[b][:].indirect(half_list(n5_l, a)), ds[b][:, a * HALF : (a + 1) * HALF], ALU.add)
-                store(b, a)
+        def finish(b, a):
+            cols = slice(a * HALF, (a + 1) * HALF)
+            nc.vector.tensor_tensor(res[b][a][:], ds[b][:, cols], far[b][a][:], ALU.subtract)
+            nc.sync.dma_start(out[P * b : P * (b + 1), cols], res[b][a][:])
 
-        def finish_split(b):
-            for a in range(2):
-                cols = slice(a * HALF, (a + 1) * HALF)
-                s_gather(aux[b][:, cols], ds[b][:].indirect(half_list(n5_l, a)))
-                nc.vector.tensor_tensor(res[b][a][:], ds[b][:, cols], aux[b][:, cols], ALU.subtract)
-                store(b, a)
-
-        nc.scalar.copy(ds[0][:], h_bank[0][:])
-        nc.vector.tensor_copy(ds[1][:], h_bank[1][:])
-        s_gather(pa[0][:], ds[0][:].indirect(n3_l[:]))
-        v_gather(pb[0][:], ds[0][:].indirect(n4_l[:]))
-        larger(0)
+        nc.vector.tensor_copy(ds[0][:], h_bank[0][:])
+        nc.scalar.copy(ds[1][:], h_bank[1][:])
+        fetch_a(0)
+        s_gather(pb[0][:], ds[0][:].indirect(n4_l[:]))
         nc.scalar.copy(ds[2][:], h_bank[2][:])
+        nc.scalar.copy(ds[3][:], h_bank[3][:])
+        fetch_a(1)
+        larger(0)
         put(0)
-        v_gather(pa[1][:], ds[1][:].indirect(n3_l[:]))
-        v_gather(pb[1][:], ds[1][:].indirect(n4_l[:]))
-        larger(1)
-        put(1)
-        nc.vector.tensor_copy(ds[3][:], h_bank[3][:])
-        for b in (2, 3):
-            v_gather(pa[b][:], ds[b][:].indirect(n3_l[:]))
-            v_gather(pb[b][:], ds[b][:].indirect(n4_l[:]))
+        for b in (1, 2):
+            fetch_b(b)
+            fetch_a(b + 1)
             larger(b)
             put(b)
-        finish_fused(0)
-        finish_fused(1)
-        finish_fused(2)
-        finish_split(3)
+        fetch_b(3)
+        fetch(v_gather, 0, 0)
+        larger(3)
+        fetch(s_gather, 1, 1)
+        fetch(s_gather, 2, 0)
+        put(3)
+        fetch(v_gather, 0, 1)
+        finish(0, 0)
+        fetch(v_gather, 1, 0)
+        finish(0, 1)
+        finish(1, 1)
+        finish(1, 0)
+        finish(2, 0)
+        for b, a in ((2, 1), (3, 0), (3, 1)):
+            fetch(s_gather, b, a)
+            finish(b, a)

@@ -19,6 +19,7 @@ ACT = mybir.ActivationFunctionType
 P = 128
 PACK = 4
 HALF = S // 2
+LAST_SPLIT = 176
 
 
 def tile_picked_dwmemgfillm_none_p_kernel(
@@ -127,8 +128,8 @@ def tile_picked_dwmemgfillm_none_p_kernel(
         def product(a, t):
             nc.vector.tensor_tensor(z[a][:, t, :], gs[t][:].indirect(half_list(n2_l, a)), sg[a][t][:], ALU.mult)
 
-        def weave(copy, a):
-            copy(zb[a][:].rearrange("p (c i) t -> p c t i", i=4), z[a][:].rearrange("p t (c i) -> p c t i", i=4))
+        def weave(copy, a, cols):
+            copy(zb[a][:, cols, :].rearrange("p (c i) t -> p c t i", i=4), z[a][:, :, cols].rearrange("p t (c i) -> p c t i", i=4))
 
         def quantise(a):
             cols = slice(a * HALF, (a + 1) * HALF)
@@ -149,16 +150,27 @@ def tile_picked_dwmemgfillm_none_p_kernel(
 
         for t in range(PACK):
             s_leaves_psum(t)
-        for a, t in ((0, 0), (1, 0), (0, 1), (1, 1), (0, 2), (0, 3), (1, 2), (1, 3)):
-            gate(a, t)
-            product(a, t)
-        weave(nc.scalar.copy, 0)
-        weave(nc.vector.tensor_copy, 1)
+        for t in range(PACK):
+            gate(0, t)
+            product(0, t)
+        gate(1, 0)
+        product(1, 0)
+        weave(nc.vector.tensor_copy, 0, slice(0, HALF))
+        gate(1, 1)
+        product(1, 1)
         quantise(0)
+        gate(1, 2)
+        product(1, 2)
+        gate(1, 3)
+        last = keep.tile([P, HALF], F32)
+        nc.scalar.activation(out=last[:], in_=gs[3][:].indirect(half_list(n2_l, 1)), func=ACT.Copy)
+        nc.vector.tensor_tensor(z[1][:, 3, :], last[:], sg[1][3][:], ALU.mult)
+        weave(nc.vector.tensor_copy, 1, slice(0, LAST_SPLIT))
+        weave(nc.scalar.copy, 1, slice(LAST_SPLIT, HALF))
         quantise(1)
 
-        for b in range(N // P):
-            for a in range(2):
+        for a in range(2):
+            for b in range(N // P):
                 cols = slice(a * HALF, (a + 1) * HALF)
                 nc.tensor.matmul_mx(
                     out=h_bank[b][:, cols], lhsT=w1_w[:, 2 * P * b : 2 * P * (b + 1)].bitcast(FP4X4), lhsT_scale=w1_sc[:, P * b : P * (b + 1)],
@@ -215,16 +227,15 @@ def tile_picked_dwmemgfillm_none_p_kernel(
         fetch_b(3)
         fetch(v_gather, 0, 0)
         larger(3)
-        fetch(s_gather, 1, 1)
-        fetch(s_gather, 2, 0)
         put(3)
-        fetch(v_gather, 0, 1)
-        finish(0, 0)
-        fetch(v_gather, 1, 0)
-        finish(0, 1)
-        finish(1, 1)
-        finish(1, 0)
+        pending = (0, 0)
+        for b, a in ((0, 1), (1, 0), (1, 1), (2, 0)):
+            fetch(v_gather, b, a)
+            finish(*pending)
+            pending = (b, a)
+        fetch(s_gather, 2, 1)
+        finish(2, 1)
         finish(2, 0)
-        for b, a in ((2, 1), (3, 0), (3, 1)):
-            fetch(s_gather, b, a)
-            finish(b, a)
+        for a in range(2):
+            fetch(s_gather, 3, a)
+            finish(3, a)

@@ -207,7 +207,8 @@ def tile_picked_dwmemgfillm_none_p_kernel(
 
         def finish(b, a):
             cols = slice(a * HALF, (a + 1) * HALF)
-            nc.vector.tensor_tensor(res[b][a][:], ds[b][:, cols], far[b][a][:], ALU.subtract)
+            engine = nc.gpsimd if b == 0 else nc.vector
+            engine.tensor_tensor(res[b][a][:], ds[b][:, cols], far[b][a][:], ALU.subtract)
             nc.sync.dma_start(out[P * b : P * (b + 1), cols], res[b][a][:])
 
         nc.vector.tensor_copy(ds[0][:], h_bank[0][:])
@@ -229,13 +230,11 @@ def tile_picked_dwmemgfillm_none_p_kernel(
         larger(3)
         put(3)
         pending = (0, 0)
-        for b, a in ((0, 1), (1, 0), (1, 1), (2, 0)):
+        for b, a in ((0, 1), (1, 0), (1, 1), (2, 0), (2, 1)):
             fetch(v_gather, b, a)
             finish(*pending)
             pending = (b, a)
-        fetch(s_gather, 2, 1)
         finish(2, 1)
-        finish(2, 0)
         for a in range(2):
             fetch(s_gather, 3, a)
             finish(3, a)

from contextlib import ExitStack

import concourse.mybir as mybir

K, T, S, N, G, H, W = 512, 1024, 512, 512, 2048, 512, 256
FLOPS = 3 * 2 * 512 * 512 * 512

F32 = mybir.dt.float32
BF16 = mybir.dt.bfloat16
I32 = mybir.dt.int32
U32 = mybir.dt.uint32
U16 = mybir.dt.uint16
U8 = mybir.dt.uint8
FP8X4 = mybir.dt.float8_e4m3fn_x4
FP4X4 = mybir.dt.float4_e2m1fn_x4
ALU = mybir.AluOpType
ACT = mybir.ActivationFunctionType

P = 128
PACK = 4
HALF = S // 2
LAST_SPLIT = 176


def tile_picked_dwmemgfillm_none_p_kernel(
    tc, x_words, x_scales, d_words, d_scales, sl, th, gn, w1_words, w1_scales, w2_words, w2_scales,
    offs, ci, n1, n2, two, n3, n4, n5, out,
):
    nc = tc.nc
    with ExitStack() as ctx:
        keep = ctx.enter_context(tc.tile_pool(name="keep", bufs=1))
        psum = ctx.enter_context(tc.psum_pool(name="psum", bufs=1))

        def load_list(src, name):
            lst = keep.tile(list(src.shape), U16, name=name)
            nc.sync.dma_start(lst[:], src)
            return lst

        def scale_tile(engine, src, name):
            plane = keep.tile([P, src.shape[2]], U8, name=name, align_bytes=64)
            engine.memset(plane[:].bitcast(I32), 0)
            return plane

        def load_scales(queue, plane, src):
            for q in range(4):
                queue.dma_start(plane[32 * q : 32 * q + 4, :].bitcast(I32), src[0, 4 * q : 4 * q + 4, :].bitcast(I32))

        def load_fp8_words(src, name):
            words = keep.tile([P, src.shape[2]], U32, name=name, align_bytes=64)
            nc.sync.dma_start(words[:].bitcast(I32), src[0].rearrange("p n t -> p (n t)").bitcast(I32))
            return words

        def load_fp4_words(src, name):
            words = keep.tile([P, src.shape[2]], U8, name=name, align_bytes=64)
            nc.sync.dma_start(words[:].bitcast(I32), src[0].bitcast(I32))
            return words

        def load_rows(src, name):
            col = keep.tile([P, PACK], F32, name=name)
            nc.gpsimd.dma_start(col[:], src.rearrange("(p t) o -> p (t o)", t=PACK))
            return col

        x_sc = scale_tile(nc.vector, x_scales, "x_sc")
        d_sc = scale_tile(nc.vector, d_scales, "d_sc")
        w2_sc = scale_tile(nc.vector, w2_scales, "w2_sc")
        w1_sc = scale_tile(nc.vector, w1_scales, "w1_sc")

        offs_l = load_list(offs, "offs_l")
        ci_l = load_list(ci, "ci_l")
        n1_l = load_list(n1, "n1_l")
        load_scales(nc.sync, x_sc, x_scales)
        x_w = load_fp8_words(x_words, "x_w")
        load_scales(nc.sync, d_sc, d_scales)
        d_w = load_fp8_words(d_words, "d_w")
        two_l = load_list(two, "two_l")
        n2_l = load_list(n2, "n2_l")
        load_scales(nc.sync, w2_sc, w2_scales)
        w2_w = load_fp4_words(w2_words, "w2_w")
        load_scales(nc.sync, w1_sc, w1_scales)
        w1_w = load_fp4_words(w1_words, "w1_w")
        n3_l = load_list(n3, "n3_l")
        n4_l = load_list(n4, "n4_l")
        n5_l = load_list(n5, "n5_l")
        sl_t = load_rows(sl, "sl_t")
        th_t = load_rows(th, "th_t")
        gn_t = load_rows(gn, "gn_t")
        sl_th = keep.tile([P, PACK], F32)
        bias = keep.tile([P, PACK], F32)
        nc.gpsimd.tensor_tensor(sl_th[:], sl_t[:], th_t[:], ALU.mult)
        nc.scalar.activation(out=bias[:], in_=sl_th[:], func=ACT.Copy, scale=-1.0)

        xq_s = keep.tile([P, S], U8, align_bytes=64)
        xq_w = keep.tile([P, S], U32, align_bytes=64)
        dq_s = keep.tile([P, H], U8, align_bytes=64)
        dq_w = keep.tile([P, H], U32, align_bytes=64)
        x2_s = keep.tile([P, S], U8, align_bytes=64)
        x2_w = keep.tile([P, S], U32, align_bytes=64)
        nc.vector.tensor_copy(xq_s[:], x_sc[:].indirect(offs_l[:]))
        nc.vector.tensor_copy(xq_w[:], x_w[:].indirect(offs_l[:]))
        nc.vector.tensor_copy(dq_s[:].rearrange("p (t m) -> p m t", t=PACK), d_sc[:].indirect(ci_l[:]))
        nc.vector.tensor_copy(dq_w[:].rearrange("p (t m) -> p m t", t=PACK), d_w[:].indirect(ci_l[:]))
        nc.vector.tensor_copy(x2_s[:], x_sc[:].indirect(two_l[:]))

        s_bank = [psum.tile([P, S], F32, name=f"s_bank{t}") for t in range(PACK)]
        h_bank = [psum.tile([P, S], F32, name=f"h_bank{b}") for b in range(N // P)]
        for t in range(PACK):
            cols = slice(P * t, P * (t + 1))
            nc.tensor.matmul_mx(
                out=s_bank[t][:], lhsT=dq_w[:, cols].bitcast(FP8X4), lhsT_scale=dq_s[:, cols],
                rhs=xq_w[:].bitcast(FP8X4), rhs_scale=xq_s[:], start=True, stop=True,
            )

        s = [keep.tile([P, S], F32, name=f"s{t}") for t in range(PACK)]
        gs = [keep.tile([P, S], F32, name=f"gs{t}") for t in range(PACK)]
        sg = [[keep.tile([P, HALF], F32, name=f"sg{a}_{t}") for t in range(PACK)] for a in range(2)]
        z = [keep.tile([P, PACK, HALF], F32, name=f"z{a}") for a in range(2)]
        zb = [keep.tile([P, HALF, PACK], BF16, name=f"zb{a}", align_bytes=64) for a in range(2)]
        zq_w = keep.tile([P, S], U32, align_bytes=64)
        zq_s = keep.tile([P, S], U8, align_bytes=64)

        def half_list(lst, a):
            return lst[:, a * HALF // 16 : (a + 1) * HALF // 16]

        def gate(a, t):
            nc.scalar.activation(out=sg[a][t][:], in_=s[t][:].indirect(half_list(n1_l, a)), func=ACT.Sigmoid,
                                 scale=sl_t[:, t : t + 1], bias=bias[:, t : t + 1])

        def product(a, t):
            nc.vector.tensor_tensor(z[a][:, t, :], gs[t][:].indirect(half_list(n2_l, a)), sg[a][t][:], ALU.mult)

        def weave(copy, a, cols):
            copy(zb[a][:, cols, :].rearrange("p (c i) t -> p c t i", i=4), z[a][:, :, cols].rearrange("p t (c i) -> p c t i", i=4))

        def quantise(a):
            cols = slice(a * HALF, (a + 1) * HALF)
            nc.vector.quantize_mx(out=zq_w[:, cols].bitcast(FP8X4), scales=zq_s[:, cols], in_=zb[a][:].rearrange("p c t -> p (c t)"))

        nc.vector.tensor_copy(x2_w[:], x_w[:].indirect(two_l[:]))
        for b in range(N // P):
            nc.tensor.matmul_mx(
                out=h_bank[b][:], lhsT=w2_w[:, 2 * P * b : 2 * P * (b + 1)].bitcast(FP4X4), lhsT_scale=w2_sc[:, P * b : P * (b + 1)],
                rhs=x2_w[:].bitcast(FP8X4), rhs_scale=x2_s[:], start=True, stop=False,
            )
        def s_leaves_psum(t):
            if t < 2:
                nc.scalar.activation(out=s[t][:], in_=s_bank[t][:], func=ACT.Copy, scale=0.0625)
            else:
                nc.vector.tensor_scalar(out=s[t][:], in0=s_bank[t][:], scalar1=0.0625, scalar2=None, op0=ALU.mult)
            nc.gpsimd.tensor_scalar(out=gs[t][:], in0=s[t][:], scalar1=gn_t[:, t : t + 1], scalar2=0.0, op0=ALU.mult, op1=ALU.add)

        for t in range(PACK):
            s_leaves_psum(t)
        for t in range(PACK):
            gate(0, t)
            product(0, t)
        gate(1, 0)
        product(1, 0)
        weave(nc.vector.tensor_copy, 0, slice(0, HALF))
        gate(1, 1)
        product(1, 1)
        quantise(0)
        gate(1, 2)
        product(1, 2)
        gate(1, 3)
        last = keep.tile([P, HALF], F32)
        nc.scalar.activation(out=last[:], in_=gs[3][:].indirect(half_list(n2_l, 1)), func=ACT.Copy)
        nc.vector.tensor_tensor(z[1][:, 3, :], last[:], sg[1][3][:], ALU.mult)
        weave(nc.vector.tensor_copy, 1, slice(0, LAST_SPLIT))
        weave(nc.scalar.copy, 1, slice(LAST_SPLIT, HALF))
        quantise(1)

        for a in range(2):
            for b in range(N // P):
                cols = slice(a * HALF, (a + 1) * HALF)
                nc.tensor.matmul_mx(
                    out=h_bank[b][:, cols], lhsT=w1_w[:, 2 * P * b : 2 * P * (b + 1)].bitcast(FP4X4), lhsT_scale=w1_sc[:, P * b : P * (b + 1)],
                    rhs=zq_w[:, cols].bitcast(FP8X4), rhs_scale=zq_s[:, cols], start=False, stop=(a == 1),
                )

        ds = [keep.tile([P, S], F32, name=f"ds{b}") for b in range(4)]
        ra = [keep.tile([P, W], F32, name=f"ra{b}") for b in range(4)]
        pa = [keep.tile([P, W], F32, name=f"pa{b}") for b in range(4)]
        pb = [keep.tile([P, W], F32, name=f"pb{b}") for b in range(4)]
        far = [[keep.tile([P, HALF], F32, name=f"far{b}_{a}") for a in range(2)] for b in range(4)]
        res = [[keep.tile([P, HALF], F32, name=f"res{b}_{a}") for a in range(2)] for b in range(4)]

        def v_gather(o, win):
            nc.vector.tensor_copy(o, win)

        def s_gather(o, win):
            nc.scalar.activation(out=o, in_=win, func=ACT.Copy)

        def fetch_a(b):
            v_gather(pa[b][:], ds[b][:].indirect(n3_l[:]))

        def fetch_b(b):
            v_gather(pb[b][:], ds[b][:].indirect(n4_l[:]))

        def larger(b):
            nc.vector.tensor_tensor(ra[b][:], pa[b][:], pb[b][:], ALU.max)

        def put(b):
            nc.scalar.activation(out=ds[b][:].indirect(n3_l[:]), in_=ra[b][:], func=ACT.Copy)

        def fetch(gather, b, a):
            gather(far[b][a][:], ds[b][:].indirect(half_list(n5_l, a)))

        def finish(b, a):
            cols = slice(a * HALF, (a + 1) * HALF)
            engine = nc.gpsimd if b == 0 else nc.vector
            engine.tensor_tensor(res[b][a][:], ds[b][:, cols], far[b][a][:], ALU.subtract)
            nc.sync.dma_start(out[P * b : P * (b + 1), cols], res[b][a][:])

        nc.vector.tensor_copy(ds[0][:], h_bank[0][:])
        nc.scalar.copy(ds[1][:], h_bank[1][:])
        fetch_a(0)
        s_gather(pb[0][:], ds[0][:].indirect(n4_l[:]))
        nc.scalar.copy(ds[2][:], h_bank[2][:])
        nc.scalar.copy(ds[3][:], h_bank[3][:])
        fetch_a(1)
        larger(0)
        put(0)
        for b in (1, 2):
            fetch_b(b)
            fetch_a(b + 1)
            larger(b)
            put(b)
        fetch_b(3)
        fetch(v_gather, 0, 0)
        larger(3)
        put(3)
        pending = (0, 0)
        for b, a in ((0, 1), (1, 0), (1, 1), (2, 0), (2, 1)):
            fetch(v_gather, b, a)
            finish(*pending)
            pending = (b, a)
        finish(2, 1)
        for a in range(2):
            fetch(s_gather, 3, a)
            finish(3, a)
